import numpy as np
import ml_dtypes


def mxq(x, axis, fmt="e4m3"):
    dtype, down = {"e4m3": (ml_dtypes.float8_e4m3fn, 7), "e5m2": (ml_dtypes.float8_e5m2, 14)}[fmt]
    v = np.moveaxis(np.asarray(x, np.float32).astype(ml_dtypes.bfloat16).astype(np.float64), axis, -1)
    blocks = v.reshape(v.shape[:-1] + (-1, 32))
    amax = np.abs(blocks).max(-1, keepdims=True)
    byte = np.maximum(np.where(amax > 0, np.frexp(amax)[1] - 1 + 127, 0) - down, 1)
    scale = np.exp2(byte - 127.0)
    codes = (blocks / scale).astype(np.float32).astype(dtype).astype(np.float64)
    return np.moveaxis((codes * scale).reshape(v.shape), -1, axis)


WIDE = False


def mx_kscale(k):
    if not WIDE:
        return np.ones(k)
    levels = np.array([30, -30])
    if k % 512:
        return np.exp2(np.random.permutation(np.resize(levels, k // 32))).repeat(32)
    a = np.empty((k // 512, 16))
    for p in range(k // 512):
        a[p, :8] = np.random.permutation(np.resize(levels, 8))
        for g in range(8):
            far = levels[np.abs(levels - a[p, g]) >= 10]
            a[p, g + 8] = far[np.random.randint(len(far))]
    return np.exp2(a.ravel()).repeat(32)


BF16 = ml_dtypes.bfloat16


def bf(x):
    return np.asarray(x, np.float32).astype(BF16)


def f64(x):
    return np.asarray(x).astype(np.float64)


M, D, F, A = 1024, 1024, 2048, 1536


def setup_inputs():
    s, t = mx_kscale(F), mx_kscale(A)
    x = (np.random.standard_normal((M, D)) + 1.0) * np.exp(0.3 * np.random.standard_normal((M, 1)))
    r = 1.0 / np.sqrt((x * x).mean(axis=1, keepdims=True))
    dy = np.random.standard_t(4, (M, F)) / np.sqrt(2.0)
    err = np.random.uniform(-1.0, 1.0, (M, A))
    w = np.random.standard_normal((D, F)) / np.sqrt(F)
    v = (np.random.standard_normal((D, A)) + np.random.standard_normal((1, A))) / np.sqrt(A)
    return {"dy": bf(dy * s), "w": bf(w / s),
            "err": bf(err * t), "v": bf(v / t),
            "gain": bf(1.0 + 0.1 * np.random.standard_normal(D)),
            "xhat": bf(x * r), "rinv": bf(r)}


def reference(dy, w, err, v, gain, xhat, rinv):
    main = mxq(f64(dy), 1, "e5m2") @ mxq(f64(w), 1, "e4m3").T
    aux = mxq(f64(err), 1, "e4m3") @ mxq(f64(v), 1, "e4m3").T
    dn = (main + aux) * f64(gain)
    xh = f64(xhat)
    c = (dn * xh).mean(axis=1, keepdims=True)
    return f64(rinv) * (dn - xh * c)

from contextlib import ExitStack

import concourse.mybir as mybir
from concourse.masks import make_identity

M, D, F, A = 1024, 1024, 2048, 1536
FLOPS = 2 * M * D * (F + A)

F32 = mybir.dt.float32
BF16 = mybir.dt.bfloat16
U32 = mybir.dt.uint32
U8 = mybir.dt.uint8
E4M3 = mybir.dt.float8_e4m3fn_x4
E5M2 = mybir.dt.float8_e5m2_x4
MULT = mybir.AluOpType.mult
ADD = mybir.AluOpType.add

P = 128
K_PASS = 512
CHUNK_WORDS = K_PASS // 2
N_HALF = 512
MAIN_PASSES = F // K_PASS
AUX_PASSES = A // K_PASS
PASSES = MAIN_PASSES + AUX_PASSES
TILES = M // P
FIRST_TILES = 2
LAST_PIECES = 4


def tile_rmsnorm_two_head_backward_s2_kernel(tc, dy, w, err, v, gain, xhat, rinv, out):
    nc = tc.nc
    dy_t = dy.rearrange("(p t) k -> p t k", t=TILES)
    err_t = err.rearrange("(p t) k -> p t k", t=TILES)
    xhat_t = xhat.rearrange("(p t) d -> p t d", t=TILES)
    out_t = out.rearrange("(p t) d -> p t d", t=TILES)
    w_t = w.rearrange("(j p) k -> p j k", p=P)
    v_t = v.rearrange("(j p) k -> p j k", p=P)

    with ExitStack() as ctx:
        keep = ctx.enter_context(tc.tile_pool(name="keep", bufs=1))
        work = ctx.enter_context(tc.tile_pool(name="work", bufs=2))
        psum = ctx.enter_context(tc.psum_pool(name="psum", bufs=1))
        ctx.enter_context(tc.manual_schedule())

        def load(pool, src, chunks, tag, bufs):
            raw = pool.tile([P, chunks * K_PASS], BF16, name=tag, tag=tag, bufs=bufs)
            if len(src.shape) == 3:
                nc.sync.dma_start(out=raw[:].rearrange("p (c k) -> p c k", c=chunks), in_=src)
            else:
                nc.sync.dma_start(out=raw[:], in_=src)
            return raw

        def pass_cols(g):
            g0 = g if g < MAIN_PASSES else g - MAIN_PASSES
            return slice(g0 * K_PASS, (g0 + 1) * K_PASS)

        raw_w = {}
        raw_pair = {}
        gain_row = keep.tile([P, D], BF16, name="gain_row")
        nc.vector.memset(gain_row[:], 0.0)

        def weight_pieces(g):
            return [(0, 2), (2, 2)] if g == 0 else [(0, 4)]

        def load_w(h, g):
            weight = w_t if g < MAIN_PASSES else v_t
            for c0, n in weight_pieces(g):
                rows = weight[:, 4 * h + c0 : 4 * h + c0 + n, pass_cols(g)]
                raw_w[h, g, c0] = load(keep, rows, n, "raw_w%d_%d_%d" % (h, g, c0), 1)

        for g in range(PASSES):
            act = dy_t if g < MAIN_PASSES else err_t
            load_w(0, g)
            raw_pair[g] = load(keep, act[:, 0:FIRST_TILES, pass_cols(g)], FIRST_TILES, "raw_pair_%d" % g, 1)
            if g == 0:
                nc.sync.dma_start(out=gain_row[0:1, :], in_=gain.rearrange("(o d) -> o d", o=1))
            load_w(1, g)

        raw_dy = {}
        raw_err = {}
        xh = {}

        def load_tile(m):
            raw_dy[m] = load(work, dy_t[:, m, :], MAIN_PASSES, "raw_dy", 3)
            raw_err[m] = load(work, err_t[:, m, :], AUX_PASSES, "raw_err", 3)

        def load_xhat(m):
            pair = keep.tile([P, 2, D], BF16, name="xhat_%d" % m)
            nc.sync.dma_start(out=pair[:], in_=xhat_t[:, m : m + 2, :])
            xh[m] = pair[:, 0, :]
            xh[m + 1] = pair[:, 1, :]

        rinv_raw = keep.tile([P, TILES], BF16, name="rinv_raw")
        load_tile(2)
        nc.sync.dma_start(out=rinv_raw[:], in_=rinv.rearrange("(p t) o -> p (t o)", t=TILES))
        load_tile(3)
        load_xhat(0)
        load_tile(4)
        load_xhat(2)

        ident = keep.tile([P, P], F32, name="ident")
        make_identity(nc, ident[:])
        ones = keep.tile([P, P], BF16, name="ones")
        nc.vector.memset(ones[:], 1.0)
        gain_all = keep.tile([P, D], BF16, name="gain_all")

        def spread_gain():
            gain_ps = psum.tile([P, D], BF16, name="gain_ps", tag="acc0")
            for h in range(2):
                cols = slice(h * N_HALF, (h + 1) * N_HALF)
                nc.tensor.matmul(gain_ps[:, cols], lhsT=ones[:], rhs=gain_row[:, cols], start=True, stop=True)
            nc.scalar.copy(out=gain_all[:], in_=gain_ps[:])

        def sort_words(copy, raw, chunks, tag, bufs):
            srt = work.tile([P, 2, chunks * P], F32, name=tag, tag=tag, bufs=bufs)
            copy(
                out=srt[:].rearrange("p u (b r) -> p u b r", r=8),
                in_=raw[:].bitcast(F32).rearrange("p (b u r) -> p u b r", u=2, r=8),
            )
            return srt

        def new_grouped(chunks, tag, bufs):
            grouped = work.tile([P, chunks * K_PASS], BF16, name=tag, tag=tag, bufs=bufs, align_bytes=64)
            return grouped

        def turn(srt, s0, grouped, c0, n):
            bank = psum.tile([P, 2, 2, P], F32, name="turn", tag="turn", bufs=4)
            for c in range(n):
                for u in range(2):
                    nc.tensor.transpose(bank[:, c, u, :], srt[:, u, (s0 + c) * P : (s0 + c + 1) * P], ident[:])
            dst = grouped[:, c0 * K_PASS : (c0 + n) * K_PASS].bitcast(F32)
            nc.scalar.copy(
                out=dst.rearrange("p (c r u) -> p c r u", c=n, u=2),
                in_=bank[:, 0:n, :, :].rearrange("p c u r -> p c r u"),
            )

        def new_codes(pool, chunks, tag, bufs):
            codes = pool.tile([P, chunks * P], U32, name=tag + "_codes", tag=tag + "_codes", bufs=bufs, align_bytes=64)
            scales = pool.tile([P, chunks * P], U8, name=tag + "_scales", tag=tag + "_scales", bufs=bufs, align_bytes=64)
            return codes, scales

        def quantize(q, grouped, fmt, c0, n):
            codes, scales = q
            nc.vector.quantize_mx(
                out=codes[:, c0 * P : (c0 + n) * P].bitcast(fmt),
                scales=scales[:, c0 * P : (c0 + n) * P],
                in_=grouped[:, c0 * K_PASS : (c0 + n) * K_PASS],
            )

        def act_format(g):
            return E5M2 if g < MAIN_PASSES else E4M3

        q_w = {}
        acc = {}

        def multiply(m, h, g, q_act, c):
            if g == 0:
                acc[m, h] = psum.tile([P, N_HALF], F32, name="acc", tag="acc%d" % (2 * (m % 2) + h))
            codes, scales = q_act
            nc.tensor.matmul_mx(
                out=acc[m, h][:],
                lhsT=codes[:, c * P : (c + 1) * P].bitcast(act_format(g)),
                lhsT_scale=scales[:, c * P : (c + 1) * P],
                rhs=q_w[h, g][0][:].bitcast(E4M3),
                rhs_scale=q_w[h, g][1][:],
                start=(g == 0),
                stop=(g == PASSES - 1),
            )

        srt_w = {}
        srt_pair = {}
        grp_w = {}
        q_pair = {}
        srt_dy = {}
        srt_err = {}
        grp_dy = {}
        grp_err = {}
        q_dy = {}
        q_err = {}

        def sort_w(h, g):
            for c0, n in weight_pieces(g):
                srt_w[h, g, c0] = sort_words(nc.vector.tensor_copy, raw_w[h, g, c0], n, "srt%d" % n, 3)

        def sort_pair(g):
            srt_pair[g] = sort_words(nc.vector.tensor_copy, raw_pair[g], FIRST_TILES, "srt2", 3)

        def turn_w(h, g):
            grp_w[h, g] = new_grouped(4, "grp4", 3)
            for c0, n in weight_pieces(g):
                for c in range(0, n, 2):
                    turn(srt_w[h, g, c0], c, grp_w[h, g], c0 + c, 2)

        def quantize_w(h, g):
            q_w[h, g] = new_codes(keep, 4, "q_w%d_%d" % (h, g), 1)
            quantize(q_w[h, g], grp_w[h, g], E4M3, 0, 4)

        def multiply_pair(g):
            for h in range(2):
                for m in range(FIRST_TILES):
                    multiply(m, h, g, q_pair[g], m)

        def sort_dy(copy, m):
            srt_dy[m] = sort_words(copy, raw_dy[m], MAIN_PASSES, "srt4", 3)

        def sort_err(copy, m):
            srt_err[m] = sort_words(copy, raw_err[m], AUX_PASSES, "srt_err", 2)

        def turn_tile(m):
            grp_dy[m] = new_grouped(MAIN_PASSES, "grp4", 3)
            grp_err[m] = new_grouped(AUX_PASSES, "grp_err", 2)
            turn(srt_dy[m], 0, grp_dy[m], 0, 2)
            turn(srt_dy[m], 2, grp_dy[m], 2, 2)
            turn(srt_err[m], 0, grp_err[m], 0, 2)
            turn(srt_err[m], 2, grp_err[m], 2, 1)

        def quantize_dy(m, c0, n):
            if m < TILES:
                if c0 == 0:
                    q_dy[m] = new_codes(work, MAIN_PASSES, "q_dy", 2)
                quantize(q_dy[m], grp_dy[m], E5M2, c0, n)

        def quantize_err(m):
            if m < TILES:
                q_err[m] = new_codes(work, AUX_PASSES, "q_err", 2)
                quantize(q_err[m], grp_err[m], E4M3, 0, 2)
                quantize(q_err[m], grp_err[m], E4M3, 2, 1)

        sort_w(0, 0)
        sort_pair(0)
        for g in range(PASSES):
            last = g == PASSES - 1
            if g > 0:
                quantize_w(1, g - 1)
            turn_w(0, g)
            if g == 0:
                sort_w(1, 0)
            if last:
                sort_dy(nc.vector.tensor_copy, FIRST_TILES)
            else:
                sort_w(0, g + 1)
            quantize_w(0, g)
            if last:
                sort_err(nc.vector.tensor_copy, FIRST_TILES)
            else:
                sort_pair(g + 1)
            grp_pair = new_grouped(FIRST_TILES, "grp_pair", 2)
            turn(srt_pair[g], 0, grp_pair, 0, FIRST_TILES)
            if g == 0:
                spread_gain()
            q_pair[g] = new_codes(work, FIRST_TILES, "q_pair", 3)
            quantize(q_pair[g], grp_pair, act_format(g), 0, FIRST_TILES)
            turn_w(1, g)
            if not last:
                sort_w(1, g + 1)
            if g > 0:
                multiply_pair(g - 1)

        rinv_f = keep.tile([P, TILES], F32, name="rinv_f")
        nc.gpsimd.tensor_copy(out=rinv_f[:], in_=rinv_raw[:])

        quantize_w(1, PASSES - 1)
        turn_tile(FIRST_TILES)
        load_tile(5)
        load_xhat(4)
        multiply_pair(PASSES - 1)

        dn = {}
        res = {}
        coef = {}

        def scale_half(m, h):
            if m >= TILES:
                return
            if h == 0:
                dn[m] = work.tile([P, D], F32, name="dn", tag="dn", bufs=3)
            cols = slice(h * N_HALF, (h + 1) * N_HALF)
            nc.vector.scalar_tensor_tensor(
                out=dn[m][:, cols], in0=acc[m, h][:], scalar=rinv_f[:, m : m + 1], in1=gain_all[:, cols], op0=MULT, op1=MULT
            )

        def row_mean(m):
            res[m] = work.tile([P, D], F32, name="res", tag="res", bufs=3)
            coef[m] = work.tile([P, 1], F32, name="coef", tag="coef", bufs=3)
            nc.vector.scalar_tensor_tensor(
                out=res[m][:], in0=dn[m][:], scalar=-1.0 / D, in1=xh[m], op0=MULT, op1=MULT, accum_out=coef[m][:]
            )

        def finish(m, pieces):
            width = D // pieces
            for i in range(pieces):
                cols = slice(i * width, (i + 1) * width)
                nc.vector.scalar_tensor_tensor(
                    out=res[m][:, cols], in0=xh[m][:, cols], scalar=coef[m][:], in1=dn[m][:, cols], op0=MULT, op1=ADD
                )
                nc.sync.dma_start(out=out_t[:, m, cols], in_=res[m][:, cols])

        def multiply_half(m, h):
            for g in range(PASSES):
                if g < MAIN_PASSES:
                    multiply(m, h, g, q_dy[m], g)
                else:
                    multiply(m, h, g, q_err[m], g - MAIN_PASSES)

        def sort_on_scalar(m):
            if m < TILES:
                sort_dy(nc.scalar.copy, m)
                sort_err(nc.scalar.copy, m)

        def load_ahead(m):
            if m < TILES:
                load_tile(m)
            if m == TILES - 1:
                load_xhat(m - 1)

        sort_on_scalar(3)
        load_ahead(6)
        sort_dy(nc.scalar.copy, 4)
        quantize_dy(2, 0, 2)
        scale_half(0, 0)
        quantize_dy(2, 2, 2)
        quantize_err(2)
        multiply_half(2, 0)
        turn_tile(3)
        sort_err(nc.scalar.copy, 4)
        load_ahead(7)
        scale_half(0, 1)
        scale_half(1, 0)
        row_mean(0)
        scale_half(1, 1)
        multiply_half(2, 1)
        finish(0, 1)
        quantize_dy(3, 0, 4)
        row_mean(1)
        quantize_err(3)
        scale_half(2, 0)
        finish(1, 1)

        for m in range(FIRST_TILES, TILES):
            scale_half(m, 1)
            if m + 2 < TILES:
                turn_tile(m + 2)
                sort_on_scalar(m + 3)
                quantize_dy(m + 2, 0, 4)
            if m + 1 < TILES:
                multiply_half(m + 1, 0)
                multiply_half(m + 1, 1)
            row_mean(m)
            quantize_err(m + 2)
            scale_half(m + 1, 0)
            finish(m, 1 if m + 1 < TILES else LAST_PIECES)
